import numpy as np
import ml_dtypes


def mxq(x, axis, fmt="e4m3"):
    dtype, down = {"e4m3": (ml_dtypes.float8_e4m3fn, 7), "e5m2": (ml_dtypes.float8_e5m2, 14)}[fmt]
    v = np.moveaxis(np.asarray(x, np.float32).astype(ml_dtypes.bfloat16).astype(np.float64), axis, -1)
    blocks = v.reshape(v.shape[:-1] + (-1, 32))
    amax = np.abs(blocks).max(-1, keepdims=True)
    byte = np.maximum(np.where(amax > 0, np.frexp(amax)[1] - 1 + 127, 0) - down, 1)
    scale = np.exp2(byte - 127.0)
    codes = (blocks / scale).astype(np.float32).astype(dtype).astype(np.float64)
    return np.moveaxis((codes * scale).reshape(v.shape), -1, axis)


WIDE = False


def mx_kscale(k):
    if not WIDE:
        return np.ones(k)
    levels = np.array([10, -10, 5, -5, 0])
    if k % 512:
        return np.exp2(np.random.permutation(np.resize(levels, k // 32))).repeat(32)
    a = np.empty((k // 512, 16))
    for p in range(k // 512):
        a[p, :8] = np.random.permutation(np.resize(levels, 8))
        for g in range(8):
            far = levels[np.abs(levels - a[p, g]) >= 10]
            a[p, g + 8] = far[np.random.randint(len(far))]
    return np.exp2(a.ravel()).repeat(32)


BF16 = ml_dtypes.bfloat16


def bf(x):
    return np.asarray(x, np.float32).astype(BF16)


def f64(x):
    return np.asarray(x).astype(np.float64)


E2M1 = np.array([0.0, 0.5, 1.0, 1.5, 2.0, 3.0, 4.0, 6.0, -0.0, -0.5, -1.0, -1.5, -2.0, -3.0, -4.0, -6.0])


def pack_weight(w, fmt):
    k, n = w.shape
    w = f64(bf(w)).reshape(k // 32, 32, n)
    amax = np.abs(w).max(1)
    if fmt == "e4m3":
        byte = np.frexp(amax)[1] - 1 + 127 - 7
    else:
        mant, ex = np.frexp(amax / 6.0)
        byte = np.where(mant > 0.5, ex, ex - 1) + 127
    byte = np.clip(np.where(amax > 0, byte, 1), 1, 254)
    scaled = (w * np.exp2(127.0 - byte)[:, None, :]).reshape(k, n).astype(np.float32)
    by_word = np.ascontiguousarray(scaled.reshape(k // 512, 128, 4, n).transpose(0, 1, 3, 2))
    if fmt == "e4m3":
        words = by_word.astype(ml_dtypes.float8_e4m3fn).view(np.uint8)
    else:
        c = by_word.astype(ml_dtypes.float4_e2m1fn).view(np.uint8) & 0xF
        words = c[..., 0::2] | (c[..., 1::2] << 4)
    return np.ascontiguousarray(words), np.ascontiguousarray(byte.astype(np.uint8).reshape(k // 512, 16, n))


def unpack_weight(words, scales, fmt):
    g, p, n, _ = words.shape
    if fmt == "e4m3":
        vals = np.ascontiguousarray(words).view(ml_dtypes.float8_e4m3fn).astype(np.float64)
    else:
        nib = np.empty((g, p, n, 4), np.uint8)
        nib[..., 0::2] = words & 0xF
        nib[..., 1::2] = words >> 4
        vals = E2M1[nib]
    vals = vals * np.repeat(np.exp2(scales.astype(np.float64) - 127.0), 8, axis=1)[..., None]
    return vals.transpose(0, 1, 3, 2).reshape(g * 512, n)
def pack4(w):
    words, scales = pack_weight(w, "e2m1")
    return words.reshape(words.shape[0], 128, -1), scales


def unpack4(words, scales):
    return unpack_weight(words.reshape(words.shape[0], 128, -1, 2), scales, "e2m1")


def planes(Y):
    n, m = Y.shape
    b = f64(bf(Y)).reshape(n // 32, 32, m)
    amax = np.abs(b).max(1)
    byte = np.clip(np.where(amax > 0, np.frexp(amax)[1] - 1 + 127 - 7, 1), 1, 254)
    codes = (b * np.exp2(127.0 - byte)[:, None, :]).reshape(n, m).astype(np.float32).astype(ml_dtypes.float8_e4m3fn).view(np.uint8)
    words = codes.reshape(n // 512, 128, 4, m).transpose(0, 1, 3, 2)
    return np.ascontiguousarray(words), np.ascontiguousarray(byte.astype(np.uint8).reshape(n // 512, 16, m))


M, F, D = 512, 2048, 1024

EPS = 0.5

def setup_inputs():
    rn = np.random.randn
    tg, tu = mx_kscale(F), mx_kscale(F)
    spread = np.exp(0.8 * rn(D))
    wg_words, wg_scales = pack4(rn(F, D) / np.sqrt(F) / tg[:, None])
    wu_words, wu_scales = pack4(rn(F, D) / np.sqrt(F) / tu[:, None])
    return {
        "rel": bf(rn(M, F)),
        "z_gate": bf(rn(M, F)),
        "z_up": bf(rn(M, F)),
        "share_gate": bf(0.5 * (1 + 0.1 * rn(F)) * tg),
        "share_up": bf(0.5 * (1 + 0.1 * rn(F)) * tu),
        "wg_words": wg_words, "wg_scales": wg_scales,
        "wu_words": wu_words, "wu_scales": wu_scales,
        "x": bf(rn(M, D) * spread),
        "rel_skip": bf(0.5 * rn(M, D) * spread),
    }

def reference(rel, z_gate, z_up, share_gate, share_up, wg_words, wg_scales, wu_words, wu_scales, x, rel_skip):
    r, zg, zu = f64(rel), f64(z_gate), f64(z_up)
    wg = unpack4(wg_words, wg_scales)
    wu = unpack4(wu_words, wu_scales)
    msg_gate = r * f64(share_gate) / np.where(zg >= 0, zg + EPS, zg - EPS)
    msg_up = r * f64(share_up) / np.where(zu >= 0, zu + EPS, zu - EPS)
    c_gate = mxq(msg_gate, 1, "e4m3") @ wg
    c_up = mxq(msg_up, 1, "e4m3") @ wu
    y = f64(x) * (c_gate + c_up) + f64(rel_skip)
    Y = y.reshape(M, D).T
    words, scales = planes(Y)
    return y, words, scales

@@ -1,0 +1,295 @@
+from contextlib import ExitStack
+
+import concourse.mybir as mybir
+from concourse.masks import make_identity
+
+M, F, D = 512, 2048, 1024
+FLOPS = 2 * 2 * M * F * D
+
+F32 = mybir.dt.float32
+BF16 = mybir.dt.bfloat16
+I32 = mybir.dt.int32
+U32 = mybir.dt.uint32
+U8 = mybir.dt.uint8
+FP8X4 = mybir.dt.float8_e4m3fn_x4
+FP4X4 = mybir.dt.float4_e2m1fn_x4
+ALU = mybir.AluOpType
+ACT = mybir.ActivationFunctionType
+
+P = 128
+PACK = 4
+KP = P * PACK
+G = F // KP
+HALF = 256
+TILES = HALF // P
+NB = D // KP
+UNITS = (M // HALF) * G * 2
+PER_HALF = G * 2
+ETA = 2.0 ** -19
+G_TOK = 192
+
+
+def tile_gated_block_relevance_step_g4_kernel(
+    tc, rel, z_gate, z_up, share_gate, share_up, wg_words, wg_scales, wu_words, wu_scales, x, rel_skip,
+    out_0, out_1, out_2,
+):
+    nc = tc.nc
+    zs = (z_gate, z_up)
+    shares = (share_gate, share_up)
+    w_words = (wg_words, wu_words)
+    w_scales = (wg_scales, wu_scales)
+
+    with ExitStack() as ctx:
+        keep = ctx.enter_context(tc.tile_pool(name="keep", bufs=1))
+        work = ctx.enter_context(tc.tile_pool(name="work", bufs=3))
+        turn = ctx.enter_context(tc.psum_pool(name="turn", bufs=4))
+        accp = ctx.enter_context(tc.psum_pool(name="accp", bufs=1))
+        ctx.enter_context(tc.manual_schedule())
+
+        ident = keep.tile([P, P], F32, name="ident")
+        quarter = keep.tile([P, 1], F32, name="quarter")
+        warm = keep.tile([P, 1], F32, name="warm")
+        w_sc = keep.tile([P, 2, G, D], U8, name="w_sc", align_bytes=64)
+        w_wd = keep.tile([P, 2, G, 2 * D], U8, name="w_wd", align_bytes=64)
+        share = [keep.tile([P, G, PACK], BF16, name="share%d" % b) for b in range(2)]
+        z_sb = [keep.tile([P, TILES, KP], BF16, name="z%d" % u) for u in range(UNITS)]
+        r_sb = [keep.tile([P, TILES, KP], BF16, name="r%d" % q) for q in range(UNITS // 2)]
+        x_sb = [keep.tile([P, TILES, D], BF16, name="x%d" % h) for h in range(2)]
+        skip_sb = [keep.tile([P, TILES, D], BF16, name="skip%d" % h) for h in range(2)]
+        y_codes = keep.tile([P, NB, M], U32, name="y_codes", align_bytes=64)
+        y_sc = keep.tile([P, NB, M], U8, name="y_sc", align_bytes=64)
+
+        nc.vector.memset(quarter[:], 2.0 ** -60)
+        nc.scalar.activation(out=warm[:], in_=quarter[:], func=ACT.Ln, bias=quarter[:], scale=2.0)
+        nc.vector.memset(w_sc[:].rearrange("p b g n -> p (b g n)").bitcast(I32), 0)
+        make_identity(nc, ident[:])
+
+        def place(u):
+            return u // PER_HALF, (u % PER_HALF) // 2, u % 2
+
+        def rows(src, h, c0, c1):
+            return src[h * HALF:(h + 1) * HALF, c0:c1].rearrange("(j p) f -> p j f", p=P)
+
+        def load_z(u):
+            h, g, b = place(u)
+            nc.sync.dma_start(out=z_sb[u][:], in_=rows(zs[b], h, g * KP, (g + 1) * KP))
+            if b == 1:
+                nc.sync.dma_start(out=r_sb[u // 2][:], in_=rows(rel, h, g * KP, (g + 1) * KP))
+
+        def load_w(g):
+            for b in range(2):
+                nc.sync.dma_start(out=w_wd[:, b, g, :].bitcast(I32), in_=w_words[b][g].bitcast(I32))
+
+        for u in range(UNITS):
+            load_z(u)
+            if u == 3:
+                for b in range(2):
+                    nc.sync.dma_start(out=share[b][:], in_=shares[b].rearrange("(g p t) -> p g t", p=P, t=PACK))
+        for b in range(2):
+            for q in range(4):
+                nc.sync.dma_start(
+                    out=w_sc[32 * q:32 * q + 4, b, :, :].bitcast(I32),
+                    in_=w_scales[b][:, 4 * q:4 * q + 4, :].rearrange("g r n -> r g n").bitcast(I32),
+                )
+        for g in range(G):
+            load_w(g)
+        for h in range(2):
+            nc.sync.dma_start(out=x_sb[h][:], in_=rows(x, h, 0, D))
+            nc.sync.dma_start(out=skip_sb[h][:], in_=rows(rel_skip, h, 0, D))
+
+        share4 = [keep.tile([P, G, PACK], F32, name="share4%d" % b) for b in range(2)]
+        t = {}
+
+        def flat(ap):
+            return ap.rearrange("p a b -> p (a b)")
+
+        def sign_half(u):
+            t["m", u] = work.tile([P, TILES, KP], BF16, name="m", tag="m", bufs=2)
+            nc.vector.tensor_scalar(out=flat(t["m", u][:]), in0=flat(z_sb[u][:]), scalar1=0.0, scalar2=0.5,
+                                    op0=ALU.is_ge, op1=ALU.subtract)
+
+        def magnitude(u):
+            t["az", u] = work.tile([P, TILES, KP // 2], I32, name="az", tag="az", bufs=3)
+            nc.vector.tensor_scalar(out=t["az", u][:].rearrange("p j (w c) -> p j w c", w=2),
+                                    in0=z_sb[u][:].bitcast(I32).rearrange("p j (c w) -> p j w c", w=2), scalar1=0x7FFF7FFF,
+                                    scalar2=None, op0=ALU.bitwise_and)
+
+        def signed_rel(u):
+            t["rm", u] = z_sb[u]
+            nc.vector.tensor_tensor(out=flat(t["rm", u][:]), in0=flat(r_sb[u // 2][:]), in1=flat(t["m", u][:]), op=ALU.mult)
+
+        def turn_words(key, u):
+            words = flat(t[key, u][:]).bitcast(F32)
+            bank = turn.tile([P, 2, HALF], F32, name="bank", tag="bank")
+            t[key + "T", u] = bank
+            for j in range(TILES):
+                for w in range(2):
+                    if key == "az":
+                        src = words[:, j * HALF + w * P:j * HALF + (w + 1) * P]
+                    else:
+                        src = words[:, j * HALF + w:(j + 1) * HALF:2]
+                    nc.tensor.transpose(bank[:, w, j * P:(j + 1) * P], src, ident[:])
+
+        def halves(bank):
+            return flat(bank[:]).bitcast(BF16).rearrange("p (w k e) -> p w e k", w=2, e=2)
+
+        def inv_root(u):
+            t["a", u] = keep.tile([P, PACK, HALF], F32, name="a%d" % u)
+            nc.scalar.activation(out=t["a", u][:].rearrange("p (w e) k -> p w e k", w=2), in_=halves(t["azT", u]),
+                                 func=ACT.Ln, bias=quarter[:], scale=2.0)
+
+        def sigmoid(u):
+            nc.scalar.activation(out=flat(t["a", u][:]), in_=flat(t["a", u][:]), func=ACT.Sigmoid, scale=-1.0)
+
+        def message(u):
+            h, g, b = place(u)
+            rm_t = halves(t["rmT", u])
+            for k in range(PACK):
+                nc.vector.scalar_tensor_tensor(out=t["a", u][:, k, :], in0=t["a", u][:, k, :],
+                                               scalar=share4[b][:, g, k:k + 1], in1=rm_t[:, k // 2, k % 2, :],
+                                               op0=ALU.mult, op1=ALU.mult)
+
+        def woven(dst, u, k0, k1):
+            return (dst.rearrange("p (c i) t -> p c t i", i=4),
+                    t["a", u][:, :, k0:k1].rearrange("p t (c i) -> p c t i", i=4))
+
+        def round_above(u):
+            t["up", u] = work.tile([P, HALF, PACK], BF16, name="up", tag="up", bufs=3)
+            dst, src = woven(t["up", u][:], u, 0, HALF)
+            nc.scalar.activation(out=dst, in_=src, func=ACT.Copy, scale=0.5 * (1.0 + ETA))
+
+        def round_below_pool(u):
+            if G_TOK > 0:
+                t["dnG", u] = work.tile([P, G_TOK, PACK], BF16, name="dnG", tag="dnG", bufs=1)
+                nc.gpsimd.tensor_scalar(out=t["dnG", u][:], in0=t["a", u][:, :, 0:G_TOK].rearrange("p t k -> p k t"),
+                                        scalar1=0.5 * (1.0 - ETA), scalar2=0.0, op0=ALU.mult, op1=ALU.add)
+
+        def round_below(u):
+            t["dn", u] = work.tile([P, HALF - G_TOK, PACK], BF16, name="dn", tag="dn", bufs=3)
+            dst, src = woven(t["dn", u][:], u, G_TOK, HALF)
+            nc.vector.tensor_scalar(out=dst, in0=src, scalar1=0.5 * (1.0 - ETA), scalar2=None, op0=ALU.mult)
+
+        def join(u):
+            t["il", u] = work.tile([P, HALF, PACK], BF16, name="il", tag="il", bufs=3, align_bytes=64)
+            nc.vector.tensor_tensor(out=flat(t["il", u][:, G_TOK:HALF, :]), in0=flat(t["up", u][:, G_TOK:HALF, :]),
+                                    in1=flat(t["dn", u][:]), op=ALU.add)
+            if G_TOK > 0:
+                nc.vector.tensor_tensor(out=flat(t["il", u][:, 0:G_TOK, :]), in0=flat(t["up", u][:, 0:G_TOK, :]),
+                                        in1=flat(t["dnG", u][:]), op=ALU.add)
+
+        def quantize(u):
+            t["codes", u] = work.tile([P, HALF], U32, name="codes", tag="codes", bufs=4, align_bytes=64)
+            t["sc", u] = work.tile([P, HALF], U8, name="sc", tag="sc", bufs=4, align_bytes=64)
+            nc.vector.quantize_mx(out=t["codes", u][:].bitcast(FP8X4), scales=t["sc", u][:], in_=flat(t["il", u][:]))
+
+        banks = [(j, n) for n in range(NB) for j in range(TILES)]
+
+        def multiply(u):
+            h, g, b = place(u)
+            for i, (j, n) in enumerate(banks):
+                if u % PER_HALF == 0:
+                    t["acc", h, i] = accp.tile([P, KP], F32, name="acc", tag="acc%d" % i)
+                nc.tensor.matmul_mx(
+                    out=t["acc", h, i][:],
+                    lhsT=t["codes", u][:, j * P:(j + 1) * P].bitcast(FP8X4),
+                    lhsT_scale=t["sc", u][:, j * P:(j + 1) * P],
+                    rhs=w_wd[:, b, g, 2 * n * KP:2 * (n + 1) * KP].bitcast(FP4X4),
+                    rhs_scale=w_sc[:, b, g, n * KP:(n + 1) * KP],
+                    start=(u % PER_HALF == 0),
+                    stop=(u % PER_HALF == PER_HALF - 1),
+                )
+
+        def times_x(h, i):
+            j, n = banks[i]
+            t["cx", h, i] = work.tile([P, KP], F32, name="cx", tag="cx", bufs=4)
+            nc.vector.tensor_tensor(out=t["cx", h, i][:], in0=t["acc", h, i][:], in1=x_sb[h][:, j, n * KP:(n + 1) * KP],
+                                    op=ALU.mult)
+
+        def add_skip(h, i):
+            j, n = banks[i]
+            t["y", h, i] = work.tile([P, KP], F32, name="y", tag="y", bufs=4)
+            nc.vector.tensor_tensor(out=t["y", h, i][:], in0=t["cx", h, i][:], in1=skip_sb[h][:, j, n * KP:(n + 1) * KP],
+                                    op=ALU.add)
+            r0 = h * HALF + j * P
+            nc.sync.dma_start(out=out_0[r0:r0 + P, n * KP:(n + 1) * KP], in_=t["y", h, i][:])
+
+        def turn_y(h, i):
+            bank = turn.tile([P, PACK, P], F32, name="bank", tag="bank")
+            t["yT", h, i] = bank
+            for k in range(PACK):
+                nc.tensor.transpose(bank[:, k, :], t["y", h, i][:, k:KP:PACK], ident[:])
+
+        def round_y(h, i):
+            t["yb", h, i] = work.tile([P, P, PACK], BF16, name="yb", tag="yb", bufs=3, align_bytes=64)
+            nc.scalar.copy(out=t["yb", h, i][:], in_=t["yT", h, i][:].rearrange("p t k -> p k t"))
+
+        def quantize_y(h, i):
+            j, n = banks[i]
+            c0 = h * HALF + j * P
+            nc.vector.quantize_mx(out=y_codes[:, n, c0:c0 + P].bitcast(FP8X4), scales=y_sc[:, n, c0:c0 + P],
+                                  in_=flat(t["yb", h, i][:]))
+            if j == TILES - 1:
+                cols = slice(h * HALF, (h + 1) * HALF)
+                nc.sync.dma_start(out=out_1[n].rearrange("p m t -> p (m t)").bitcast(I32)[:, cols],
+                                  in_=y_codes[:, n, cols].bitcast(I32))
+            if i == len(banks) - 1:
+                cols = slice(h * HALF, (h + 1) * HALF)
+                for q in range(4):
+                    nc.sync.dma_start(
+                        out=out_2[:, 4 * q:4 * q + 4, cols].rearrange("g r m -> r g m").bitcast(I32),
+                        in_=y_sc[32 * q:32 * q + 4, :, cols].bitcast(I32),
+                    )
+
+        def on(fn, u, *more):
+            if 0 <= u < UNITS:
+                fn(u, *more)
+
+        def first_half(fn, i):
+            if 0 <= i < len(banks):
+                fn(0, i)
+
+        def turn_magnitude(u):
+            turn_words("az", u)
+
+        def turn_signed(u):
+            turn_words("rm", u)
+
+        for u in range(UNITS + 1):
+            on(magnitude, u)
+            on(signed_rel, u - 1)
+            on(sign_half, u)
+            on(turn_magnitude, u)
+            on(inv_root, u)
+        for b in range(2):
+            nc.vector.tensor_scalar(out=share4[b][:], in0=share[b][:], scalar1=4.0, scalar2=None, op0=ALU.mult)
+
+        add_steps = (12, 13, 14, 15)
+        for s in range(-2, UNITS + 3):
+            on(quantize, s - 3)
+            on(round_below, s - 1)
+            on(join, s - 2)
+            on(round_below_pool, s - 1)
+            on(round_above, s - 1)
+            on(sigmoid, s + 2)
+            on(message, s)
+            on(turn_signed, s + 2)
+            if s == PER_HALF + 3:
+                times_x(0, 2)
+                times_x(0, 3)
+            on(multiply, s - 3)
+            if s == PER_HALF + 2:
+                times_x(0, 0)
+                times_x(0, 1)
+            for i, s0 in enumerate(add_steps):
+                if s == s0 + 2:
+                    quantize_y(0, i)
+                if s == s0 + 1:
+                    turn_y(0, i)
+                    round_y(0, i)
+                if s == s0:
+                    add_skip(0, i)
+
+        for i in range(-1, len(banks) + 3):
+            for lag, fn in enumerate((times_x, add_skip, turn_y, round_y, quantize_y)):
+                if 0 <= i + 1 - lag < len(banks):
+                    fn(1, i + 1 - lag)

@@ -18,15 +18,21 @@ ACT = mybir.ActivationFunctionType
 
 P = 128
 PACK = 4
-KP = P * PACK
-G = F // KP
+GROUP = P * PACK
+GROUPS = F // GROUP
 HALF = 256
 TILES = HALF // P
-NB = D // KP
-UNITS = (M // HALF) * G * 2
-PER_HALF = G * 2
-ETA = 2.0 ** -19
-G_TOK = 192
+OUT_GROUPS = D // GROUP
+PAIRS = (M // HALF) * GROUPS
+PAIR_COLS = 2 * HALF
+QUADRANTS = 4
+
+ETA = 3.0 * 2.0 ** -21
+LOG_FLOOR = 2.0 ** -60
+ABS_MASK = 0x7FFF7FFF
+
+LOWER_ON_GPSIMD = (416, 416, 416, 448, 512, 416, 384)
+UPPER_ON_VECTOR = (384, 128, 0, 128, 0, 0, 0)
 
 
 def tile_gated_block_relevance_step_g4_kernel(
@@ -34,262 +40,285 @@ def tile_gated_block_relevance_step_g4_kernel(
     out_0, out_1, out_2,
 ):
     nc = tc.nc
-    zs = (z_gate, z_up)
-    shares = (share_gate, share_up)
-    w_words = (wg_words, wu_words)
-    w_scales = (wg_scales, wu_scales)
+    z_hbm = (z_gate, z_up)
+    share_hbm = (share_gate, share_up)
+    words_hbm = (wg_words, wu_words)
+    scales_hbm = (wg_scales, wu_scales)
 
     with ExitStack() as ctx:
         keep = ctx.enter_context(tc.tile_pool(name="keep", bufs=1))
         work = ctx.enter_context(tc.tile_pool(name="work", bufs=3))
         turn = ctx.enter_context(tc.psum_pool(name="turn", bufs=4))
-        accp = ctx.enter_context(tc.psum_pool(name="accp", bufs=1))
+        sums = ctx.enter_context(tc.psum_pool(name="sums", bufs=1))
         ctx.enter_context(tc.manual_schedule())
 
         ident = keep.tile([P, P], F32, name="ident")
-        quarter = keep.tile([P, 1], F32, name="quarter")
-        warm = keep.tile([P, 1], F32, name="warm")
-        w_sc = keep.tile([P, 2, G, D], U8, name="w_sc", align_bytes=64)
-        w_wd = keep.tile([P, 2, G, 2 * D], U8, name="w_wd", align_bytes=64)
-        share = [keep.tile([P, G, PACK], BF16, name="share%d" % b) for b in range(2)]
-        z_sb = [keep.tile([P, TILES, KP], BF16, name="z%d" % u) for u in range(UNITS)]
-        r_sb = [keep.tile([P, TILES, KP], BF16, name="r%d" % q) for q in range(UNITS // 2)]
+        log_floor = keep.tile([P, 1], F32, name="log_floor")
+        w_scales = keep.tile([P, 2, GROUPS, D], U8, name="w_scales", align_bytes=64)
+        w_words = keep.tile([P, 2, GROUPS, 2 * D], U8, name="w_words", align_bytes=64)
+        share = [keep.tile([P, GROUPS, PACK], BF16, name="share%d" % b) for b in range(2)]
+        pre = [keep.tile([P, 2, TILES, GROUP], BF16, name="pre%d" % q) for q in range(PAIRS)]
+        rel_sb = [keep.tile([P, TILES, GROUP], BF16, name="rel%d" % q) for q in range(PAIRS)]
         x_sb = [keep.tile([P, TILES, D], BF16, name="x%d" % h) for h in range(2)]
         skip_sb = [keep.tile([P, TILES, D], BF16, name="skip%d" % h) for h in range(2)]
-        y_codes = keep.tile([P, NB, M], U32, name="y_codes", align_bytes=64)
-        y_sc = keep.tile([P, NB, M], U8, name="y_sc", align_bytes=64)
+        y_codes = keep.tile([P, OUT_GROUPS, M], U32, name="y_codes", align_bytes=64)
+        y_scales = keep.tile([P, OUT_GROUPS, M], U8, name="y_scales", align_bytes=64)
+        share4 = [keep.tile([P, GROUPS, PACK], F32, name="share4_%d" % b) for b in range(2)]
+        value = [keep.tile([P, PACK, PAIR_COLS], F32, name="value%d" % q) for q in range(PAIRS)]
+        y_sb = [keep.tile([P, OUT_GROUPS, TILES, GROUP], F32, name="y%d" % h) for h in range(2)]
+        lower_last = keep.tile([P, PAIR_COLS, PACK], BF16, name="lower_last", align_bytes=64)
 
-        nc.vector.memset(quarter[:], 2.0 ** -60)
-        nc.scalar.activation(out=warm[:], in_=quarter[:], func=ACT.Ln, bias=quarter[:], scale=2.0)
-        nc.vector.memset(w_sc[:].rearrange("p b g n -> p (b g n)").bitcast(I32), 0)
+        nc.vector.memset(log_floor[:], LOG_FLOOR)
+        nc.vector.memset(w_scales[:].rearrange("p b g n -> p (b g n)").bitcast(I32), 0)
         make_identity(nc, ident[:])
 
-        def place(u):
-            return u // PER_HALF, (u % PER_HALF) // 2, u % 2
+        def token_rows(src, h, group):
+            return src[h * HALF:(h + 1) * HALF, group * GROUP:(group + 1) * GROUP].rearrange("(j p) f -> p j f", p=P)
 
-        def rows(src, h, c0, c1):
-            return src[h * HALF:(h + 1) * HALF, c0:c1].rearrange("(j p) f -> p j f", p=P)
-
-        def load_z(u):
-            h, g, b = place(u)
-            nc.sync.dma_start(out=z_sb[u][:], in_=rows(zs[b], h, g * KP, (g + 1) * KP))
-            if b == 1:
-                nc.sync.dma_start(out=r_sb[u // 2][:], in_=rows(rel, h, g * KP, (g + 1) * KP))
-
-        def load_w(g):
-            for b in range(2):
-                nc.sync.dma_start(out=w_wd[:, b, g, :].bitcast(I32), in_=w_words[b][g].bitcast(I32))
-
-        for u in range(UNITS):
-            load_z(u)
-            if u == 3:
+        rel_load_lag = 2
+        for q in range(PAIRS + rel_load_lag):
+            if q < PAIRS:
                 for b in range(2):
-                    nc.sync.dma_start(out=share[b][:], in_=shares[b].rearrange("(g p t) -> p g t", p=P, t=PACK))
+                    nc.sync.dma_start(out=pre[q][:, b], in_=token_rows(z_hbm[b], q // GROUPS, q % GROUPS))
+            if q >= rel_load_lag:
+                r = q - rel_load_lag
+                nc.sync.dma_start(out=rel_sb[r][:], in_=token_rows(rel, r // GROUPS, r % GROUPS))
         for b in range(2):
-            for q in range(4):
+            nc.sync.dma_start(out=share[b][:], in_=share_hbm[b].rearrange("(g p t) -> p g t", p=P, t=PACK))
+        for b in range(2):
+            for quad in range(QUADRANTS):
                 nc.sync.dma_start(
-                    out=w_sc[32 * q:32 * q + 4, b, :, :].bitcast(I32),
-                    in_=w_scales[b][:, 4 * q:4 * q + 4, :].rearrange("g r n -> r g n").bitcast(I32),
+                    out=w_scales[32 * quad:32 * quad + 4, b, :, :].bitcast(I32),
+                    in_=scales_hbm[b][:, 4 * quad:4 * quad + 4, :].rearrange("g r n -> r g n").bitcast(I32),
                 )
-        for g in range(G):
-            load_w(g)
+        for g in range(GROUPS):
+            for b in range(2):
+                nc.sync.dma_start(out=w_words[:, b, g, :].bitcast(I32), in_=words_hbm[b][g].bitcast(I32))
         for h in range(2):
-            nc.sync.dma_start(out=x_sb[h][:], in_=rows(x, h, 0, D))
-            nc.sync.dma_start(out=skip_sb[h][:], in_=rows(rel_skip, h, 0, D))
+            tokens = slice(h * HALF, (h + 1) * HALF)
+            nc.sync.dma_start(out=x_sb[h][:], in_=x[tokens, :].rearrange("(j p) f -> p j f", p=P))
+            nc.sync.dma_start(out=skip_sb[h][:], in_=rel_skip[tokens, :].rearrange("(j p) f -> p j f", p=P))
 
-        share4 = [keep.tile([P, G, PACK], F32, name="share4%d" % b) for b in range(2)]
-        t = {}
+        signed_t, upper, lower, codes, scales, acc, y_rounded = {}, {}, {}, {}, {}, {}, {}
 
         def flat(ap):
             return ap.rearrange("p a b -> p (a b)")
 
-        def sign_half(u):
-            t["m", u] = work.tile([P, TILES, KP], BF16, name="m", tag="m", bufs=2)
-            nc.vector.tensor_scalar(out=flat(t["m", u][:]), in0=flat(z_sb[u][:]), scalar1=0.0, scalar2=0.5,
-                                    op0=ALU.is_ge, op1=ALU.subtract)
+        def unit_cols(b):
+            return slice(b * HALF, (b + 1) * HALF)
 
-        def magnitude(u):
-            t["az", u] = work.tile([P, TILES, KP // 2], I32, name="az", tag="az", bufs=3)
-            nc.vector.tensor_scalar(out=t["az", u][:].rearrange("p j (w c) -> p j w c", w=2),
-                                    in0=z_sb[u][:].bitcast(I32).rearrange("p j (c w) -> p j w c", w=2), scalar1=0x7FFF7FFF,
-                                    scalar2=None, op0=ALU.bitwise_and)
-
-        def signed_rel(u):
-            t["rm", u] = z_sb[u]
-            nc.vector.tensor_tensor(out=flat(t["rm", u][:]), in0=flat(r_sb[u // 2][:]), in1=flat(t["m", u][:]), op=ALU.mult)
-
-        def turn_words(key, u):
-            words = flat(t[key, u][:]).bitcast(F32)
-            bank = turn.tile([P, 2, HALF], F32, name="bank", tag="bank")
-            t[key + "T", u] = bank
-            for j in range(TILES):
-                for w in range(2):
-                    if key == "az":
-                        src = words[:, j * HALF + w * P:j * HALF + (w + 1) * P]
-                    else:
-                        src = words[:, j * HALF + w:(j + 1) * HALF:2]
-                    nc.tensor.transpose(bank[:, w, j * P:(j + 1) * P], src, ident[:])
-
-        def halves(bank):
+        def bank_values(bank):
             return flat(bank[:]).bitcast(BF16).rearrange("p (w k e) -> p w e k", w=2, e=2)
 
-        def inv_root(u):
-            t["a", u] = keep.tile([P, PACK, HALF], F32, name="a%d" % u)
-            nc.scalar.activation(out=t["a", u][:].rearrange("p (w e) k -> p w e k", w=2), in_=halves(t["azT", u]),
-                                 func=ACT.Ln, bias=quarter[:], scale=2.0)
+        def log_magnitude(q, b):
+            magnitude = work.tile([P, TILES, 2, P], I32, name="magnitude", tag="magnitude")
+            nc.vector.tensor_scalar(out=magnitude[:],
+                                    in0=pre[q][:, b].bitcast(I32).rearrange("p j (c w) -> p j w c", w=2),
+                                    scalar1=ABS_MASK, scalar2=None, op0=ALU.bitwise_and)
+            bank = turn.tile([P, 2, HALF], F32, name="bank", tag="bank")
+            for j in range(TILES):
+                for w in range(2):
+                    nc.tensor.transpose(bank[:, w, j * P:(j + 1) * P], magnitude[:, j, w, :].bitcast(F32), ident[:])
+            nc.scalar.activation(out=value[q][:, :, unit_cols(b)].rearrange("p (w e) k -> p w e k", w=2),
+                                 in_=bank_values(bank), func=ACT.Ln, bias=log_floor[:], scale=2.0)
 
-        def sigmoid(u):
-            nc.scalar.activation(out=flat(t["a", u][:]), in_=flat(t["a", u][:]), func=ACT.Sigmoid, scale=-1.0)
+        def half_sign(q):
+            z = pre[q][:].rearrange("p b j f -> p (b j f)")
+            nc.vector.tensor_scalar(out=z, in0=z, scalar1=0.0, scalar2=0.5, op0=ALU.is_ge, op1=ALU.subtract)
 
-        def message(u):
-            h, g, b = place(u)
-            rm_t = halves(t["rmT", u])
-            for k in range(PACK):
-                nc.vector.scalar_tensor_tensor(out=t["a", u][:, k, :], in0=t["a", u][:, k, :],
-                                               scalar=share4[b][:, g, k:k + 1], in1=rm_t[:, k // 2, k % 2, :],
-                                               op0=ALU.mult, op1=ALU.mult)
+        def signed_rel(q):
+            sign = pre[q][:].rearrange("p b j f -> p b (j f)")
+            rel_twice = flat(rel_sb[q][:]).unsqueeze(1).to_broadcast([P, 2, TILES * GROUP])
+            nc.vector.tensor_tensor(out=sign, in0=sign, in1=rel_twice, op=ALU.mult)
 
-        def woven(dst, u, k0, k1):
-            return (dst.rearrange("p (c i) t -> p c t i", i=4),
-                    t["a", u][:, :, k0:k1].rearrange("p t (c i) -> p c t i", i=4))
+        def sigmoid(ap):
+            nc.scalar.activation(out=ap, in_=ap, func=ACT.Sigmoid, scale=-1.0)
 
-        def round_above(u):
-            t["up", u] = work.tile([P, HALF, PACK], BF16, name="up", tag="up", bufs=3)
-            dst, src = woven(t["up", u][:], u, 0, HALF)
-            nc.scalar.activation(out=dst, in_=src, func=ACT.Copy, scale=0.5 * (1.0 + ETA))
+        def turn_signed_rel(q):
+            for b in range(2):
+                bank = turn.tile([P, 2, HALF], F32, name="bank", tag="bank")
+                signed_t[q, b] = bank
+                for j in range(TILES):
+                    words = pre[q][:, b, j, :].bitcast(F32)
+                    for w in range(2):
+                        nc.tensor.transpose(bank[:, w, j * P:(j + 1) * P], words[:, w:GROUP // 2:2], ident[:])
 
-        def round_below_pool(u):
-            if G_TOK > 0:
-                t["dnG", u] = work.tile([P, G_TOK, PACK], BF16, name="dnG", tag="dnG", bufs=1)
-                nc.gpsimd.tensor_scalar(out=t["dnG", u][:], in0=t["a", u][:, :, 0:G_TOK].rearrange("p t k -> p k t"),
-                                        scalar1=0.5 * (1.0 - ETA), scalar2=0.0, op0=ALU.mult, op1=ALU.add)
+        def message(q, b):
+            signed = bank_values(signed_t[q, b])
+            for t in range(PACK):
+                plane = value[q][:, t, unit_cols(b)]
+                nc.vector.scalar_tensor_tensor(out=plane, in0=plane, scalar=share4[b][:, q % GROUPS, t:t + 1],
+                                               in1=signed[:, t // 2, t % 2, :], op0=ALU.mult, op1=ALU.mult)
 
-        def round_below(u):
-            t["dn", u] = work.tile([P, HALF - G_TOK, PACK], BF16, name="dn", tag="dn", bufs=3)
-            dst, src = woven(t["dn", u][:], u, G_TOK, HALF)
-            nc.vector.tensor_scalar(out=dst, in0=src, scalar1=0.5 * (1.0 - ETA), scalar2=None, op0=ALU.mult)
+        def round_scaled(dst, q, c0, c1, factor, engine):
+            if engine == "gpsimd":
+                nc.gpsimd.tensor_scalar(out=dst[:, c0:c1, :], in0=value[q][:, :, c0:c1].rearrange("p t k -> p k t"),
+                                        scalar1=factor, scalar2=0.0, op0=ALU.mult, op1=ALU.add)
+                return
+            out = dst[:, c0:c1, :].rearrange("p (c i) t -> p c t i", i=4)
+            src = value[q][:, :, c0:c1].rearrange("p t (c i) -> p c t i", i=4)
+            if engine == "scalar":
+                nc.scalar.activation(out=out, in_=src, func=ACT.Copy, scale=factor)
+            else:
+                nc.vector.tensor_scalar(out=out, in0=src, scalar1=factor, scalar2=None, op0=ALU.mult)
 
-        def join(u):
-            t["il", u] = work.tile([P, HALF, PACK], BF16, name="il", tag="il", bufs=3, align_bytes=64)
-            nc.vector.tensor_tensor(out=flat(t["il", u][:, G_TOK:HALF, :]), in0=flat(t["up", u][:, G_TOK:HALF, :]),
-                                    in1=flat(t["dn", u][:]), op=ALU.add)
-            if G_TOK > 0:
-                nc.vector.tensor_tensor(out=flat(t["il", u][:, 0:G_TOK, :]), in0=flat(t["up", u][:, 0:G_TOK, :]),
-                                        in1=flat(t["dnG", u][:]), op=ALU.add)
+        def round_upper(q, c0, c1, engine):
+            if c0 == 0:
+                upper[q] = work.tile([P, PAIR_COLS, PACK], BF16, name="upper", tag="upper", bufs=2, align_bytes=64)
+            if c0 < c1:
+                round_scaled(upper[q], q, c0, c1, 0.5 * (1.0 + ETA), engine)
 
-        def quantize(u):
-            t["codes", u] = work.tile([P, HALF], U32, name="codes", tag="codes", bufs=4, align_bytes=64)
-            t["sc", u] = work.tile([P, HALF], U8, name="sc", tag="sc", bufs=4, align_bytes=64)
-            nc.vector.quantize_mx(out=t["codes", u][:].bitcast(FP8X4), scales=t["sc", u][:], in_=flat(t["il", u][:]))
+        def round_lower(q, c0, c1, engine):
+            if c0 < c1:
+                round_scaled(lower[q], q, c0, c1, 0.5 * (1.0 - ETA), engine)
 
-        banks = [(j, n) for n in range(NB) for j in range(TILES)]
+        def round_lower_shared(q):
+            lower[q] = work.tile([P, PAIR_COLS, PACK], BF16, name="lower", tag="lower", bufs=1, align_bytes=64)
+            round_lower(q, LOWER_ON_GPSIMD[q], PAIR_COLS, "scalar")
+            round_lower(q, 0, LOWER_ON_GPSIMD[q], "gpsimd")
 
-        def multiply(u):
-            h, g, b = place(u)
+        def join(q, b):
+            total = flat(lower[q][:, unit_cols(b), :])
+            nc.vector.tensor_tensor(out=total, in0=flat(upper[q][:, unit_cols(b), :]), in1=total, op=ALU.add)
+
+        def quantize(q, b):
+            if b == 0:
+                codes[q] = work.tile([P, PAIR_COLS], U32, name="codes", tag="codes", align_bytes=64)
+                scales[q] = work.tile([P, PAIR_COLS], U8, name="scales", tag="scales", align_bytes=64)
+            nc.vector.quantize_mx(out=codes[q][:, unit_cols(b)].bitcast(FP8X4), scales=scales[q][:, unit_cols(b)],
+                                  in_=flat(lower[q][:, unit_cols(b), :]))
+
+        def join_and_quantize(q):
+            for step in (join, quantize):
+                for b in range(2):
+                    step(q, b)
+
+        banks = [(j, n) for n in range(OUT_GROUPS) for j in range(TILES)]
+
+        def multiply(q):
+            h, g = divmod(q, GROUPS)
             for i, (j, n) in enumerate(banks):
-                if u % PER_HALF == 0:
-                    t["acc", h, i] = accp.tile([P, KP], F32, name="acc", tag="acc%d" % i)
-                nc.tensor.matmul_mx(
-                    out=t["acc", h, i][:],
-                    lhsT=t["codes", u][:, j * P:(j + 1) * P].bitcast(FP8X4),
-                    lhsT_scale=t["sc", u][:, j * P:(j + 1) * P],
-                    rhs=w_wd[:, b, g, 2 * n * KP:2 * (n + 1) * KP].bitcast(FP4X4),
-                    rhs_scale=w_sc[:, b, g, n * KP:(n + 1) * KP],
-                    start=(u % PER_HALF == 0),
-                    stop=(u % PER_HALF == PER_HALF - 1),
-                )
+                if g == 0:
+                    acc[h, i] = sums.tile([P, GROUP], F32, name="acc", tag="acc%d" % i)
+                for b in range(2):
+                    tokens = slice(b * HALF + j * P, b * HALF + (j + 1) * P)
+                    nc.tensor.matmul_mx(
+                        out=acc[h, i][:],
+                        lhsT=codes[q][:, tokens].bitcast(FP8X4),
+                        lhsT_scale=scales[q][:, tokens],
+                        rhs=w_words[:, b, g, 2 * n * GROUP:2 * (n + 1) * GROUP].bitcast(FP4X4),
+                        rhs_scale=w_scales[:, b, g, n * GROUP:(n + 1) * GROUP],
+                        start=(g == 0 and b == 0),
+                        stop=(g == GROUPS - 1 and b == 1),
+                    )
 
         def times_x(h, i):
             j, n = banks[i]
-            t["cx", h, i] = work.tile([P, KP], F32, name="cx", tag="cx", bufs=4)
-            nc.vector.tensor_tensor(out=t["cx", h, i][:], in0=t["acc", h, i][:], in1=x_sb[h][:, j, n * KP:(n + 1) * KP],
-                                    op=ALU.mult)
+            nc.vector.tensor_tensor(out=y_sb[h][:, n, j, :], in0=acc[h, i][:],
+                                    in1=x_sb[h][:, j, n * GROUP:(n + 1) * GROUP], op=ALU.mult)
 
-        def add_skip(h, i):
-            j, n = banks[i]
-            t["y", h, i] = work.tile([P, KP], F32, name="y", tag="y", bufs=4)
-            nc.vector.tensor_tensor(out=t["y", h, i][:], in0=t["cx", h, i][:], in1=skip_sb[h][:, j, n * KP:(n + 1) * KP],
-                                    op=ALU.add)
-            r0 = h * HALF + j * P
-            nc.sync.dma_start(out=out_0[r0:r0 + P, n * KP:(n + 1) * KP], in_=t["y", h, i][:])
+        def add_skip_and_store(h, n, j0, j1, engine):
+            y = y_sb[h][:, n, j0:j1, :]
+            engine.tensor_tensor(out=y, in0=y, in1=skip_sb[h][:, j0:j1, n * GROUP:(n + 1) * GROUP], op=ALU.add)
+            nc.sync.dma_start(out=token_rows(out_0, h, n)[:, j0:j1, :], in_=y)
 
         def turn_y(h, i):
-            bank = turn.tile([P, PACK, P], F32, name="bank", tag="bank")
-            t["yT", h, i] = bank
-            for k in range(PACK):
-                nc.tensor.transpose(bank[:, k, :], t["y", h, i][:, k:KP:PACK], ident[:])
-
-        def round_y(h, i):
-            t["yb", h, i] = work.tile([P, P, PACK], BF16, name="yb", tag="yb", bufs=3, align_bytes=64)
-            nc.scalar.copy(out=t["yb", h, i][:], in_=t["yT", h, i][:].rearrange("p t k -> p k t"))
-
-        def quantize_y(h, i):
             j, n = banks[i]
-            c0 = h * HALF + j * P
-            nc.vector.quantize_mx(out=y_codes[:, n, c0:c0 + P].bitcast(FP8X4), scales=y_sc[:, n, c0:c0 + P],
-                                  in_=flat(t["yb", h, i][:]))
-            if j == TILES - 1:
-                cols = slice(h * HALF, (h + 1) * HALF)
-                nc.sync.dma_start(out=out_1[n].rearrange("p m t -> p (m t)").bitcast(I32)[:, cols],
-                                  in_=y_codes[:, n, cols].bitcast(I32))
-            if i == len(banks) - 1:
-                cols = slice(h * HALF, (h + 1) * HALF)
-                for q in range(4):
-                    nc.sync.dma_start(
-                        out=out_2[:, 4 * q:4 * q + 4, cols].rearrange("g r m -> r g m").bitcast(I32),
-                        in_=y_sc[32 * q:32 * q + 4, :, cols].bitcast(I32),
+            bank = turn.tile([P, PACK, P], F32, name="bank", tag="bank")
+            for t in range(PACK):
+                nc.tensor.transpose(bank[:, t, :], y_sb[h][:, n, j, t:GROUP:PACK], ident[:])
+            if j == 0:
+                y_rounded[h, n] = work.tile([P, HALF, PACK], BF16, name="y_rounded", tag="y_rounded", bufs=2,
+                                            align_bytes=64)
+            nc.scalar.copy(out=y_rounded[h, n][:, j * P:(j + 1) * P, :], in_=bank[:].rearrange("p t k -> p k t"))
+
+        def quantize_y(h, n, j0, j1):
+            tokens = slice(h * HALF + j0 * P, h * HALF + j1 * P)
+            nc.vector.quantize_mx(out=y_codes[:, n, tokens].bitcast(FP8X4), scales=y_scales[:, n, tokens],
+                                  in_=flat(y_rounded[h, n][:, j0 * P:j1 * P, :]))
+            if j1 < TILES:
+                return
+            half = slice(h * HALF, (h + 1) * HALF)
+            nc.sync.dma_start(out=out_1[n].rearrange("p m t -> p (m t)").bitcast(I32)[:, half],
+                              in_=y_codes[:, n, half].bitcast(I32))
+            if n == OUT_GROUPS - 1:
+                for quad in range(QUADRANTS):
+                    queue = nc.scalar if h == 1 and quad % 2 == 0 else nc.sync
+                    queue.dma_start(
+                        out=out_2[:, 4 * quad:4 * quad + 4, half].rearrange("g r m -> r g m").bitcast(I32),
+                        in_=y_scales[32 * quad:32 * quad + 4, :, half].bitcast(I32),
                     )
 
-        def on(fn, u, *more):
-            if 0 <= u < UNITS:
-                fn(u, *more)
-
-        def first_half(fn, i):
-            if 0 <= i < len(banks):
-                fn(0, i)
-
-        def turn_magnitude(u):
-            turn_words("az", u)
-
-        def turn_signed(u):
-            turn_words("rm", u)
-
-        for u in range(UNITS + 1):
-            on(magnitude, u)
-            on(signed_rel, u - 1)
-            on(sign_half, u)
-            on(turn_magnitude, u)
-            on(inv_root, u)
+        sign_lag, product_lag = 1, 3
+        for q in range(PAIRS + product_lag):
+            if q < PAIRS:
+                log_magnitude(q, 0)
+            if q >= product_lag:
+                signed_rel(q - product_lag)
+            if q < PAIRS:
+                log_magnitude(q, 1)
+            if 0 <= q - sign_lag < PAIRS:
+                half_sign(q - sign_lag)
         for b in range(2):
             nc.vector.tensor_scalar(out=share4[b][:], in0=share[b][:], scalar1=4.0, scalar2=None, op0=ALU.mult)
 
-        add_steps = (12, 13, 14, 15)
-        for s in range(-2, UNITS + 3):
-            on(quantize, s - 3)
-            on(round_below, s - 1)
-            on(join, s - 2)
-            on(round_below_pool, s - 1)
-            on(round_above, s - 1)
-            on(sigmoid, s + 2)
-            on(message, s)
-            on(turn_signed, s + 2)
-            if s == PER_HALF + 3:
-                times_x(0, 2)
-                times_x(0, 3)
-            on(multiply, s - 3)
-            if s == PER_HALF + 2:
-                times_x(0, 0)
-                times_x(0, 1)
-            for i, s0 in enumerate(add_steps):
-                if s == s0 + 2:
-                    quantize_y(0, i)
-                if s == s0 + 1:
-                    turn_y(0, i)
-                    round_y(0, i)
-                if s == s0:
-                    add_skip(0, i)
+        last = PAIRS - 1
+        short_sigmoids = 2
+        first_half_summed = GROUPS + 1
+        sigmoid(value[0][:, 0:2, unit_cols(0)])
+        sigmoid(value[0][:, 2:4, unit_cols(0)])
+        sigmoid(value[0][:, :, unit_cols(1)])
+        turn_signed_rel(0)
+        for q in range(PAIRS):
+            if q >= 2:
+                round_upper(q - 2, PAIR_COLS - UPPER_ON_VECTOR[q - 2], PAIR_COLS, "vector")
+                join_and_quantize(q - 2)
+            if q > first_half_summed:
+                add_skip_and_store(0, q - first_half_summed - 1, 0, TILES, nc.vector)
+            if q >= 1:
+                round_lower_shared(q - 1)
+            if q + 1 <= short_sigmoids:
+                for b in range(2):
+                    sigmoid(value[q + 1][:, :, unit_cols(b)])
+            elif q < last:
+                sigmoid(flat(value[q + 1][:]))
+            if q < last:
+                turn_signed_rel(q + 1)
+            if q >= 2:
+                multiply(q - 2)
+            message(q, 0)
+            message(q, 1)
+            if q == first_half_summed + 1:
+                turn_y(0, 0)
+            if q < last:
+                round_upper(q, 0, PAIR_COLS - UPPER_ON_VECTOR[q], "scalar")
+            if q == first_half_summed + 1:
+                turn_y(0, 1)
+            if q == first_half_summed:
+                for i in range(len(banks)):
+                    times_x(0, i)
 
-        for i in range(-1, len(banks) + 3):
-            for lag, fn in enumerate((times_x, add_skip, turn_y, round_y, quantize_y)):
-                if 0 <= i + 1 - lag < len(banks):
-                    fn(1, i + 1 - lag)
+        lower[last] = lower_last
+        round_upper(last, 0, HALF, "scalar")
+        round_lower(last, 0, HALF, "scalar")
+        round_lower(last, HALF, PAIR_COLS, "scalar")
+        join_and_quantize(last - 1)
+        turn_y(0, 2)
+        turn_y(0, 3)
+        join(last, 0)
+        round_upper(last, HALF, PAIR_COLS, "vector")
+        quantize(last, 0)
+        join(last, 1)
+        quantize_y(0, 0, 0, TILES)
+        quantize(last, 1)
+        quantize_y(0, 1, 0, TILES)
+        multiply(last - 1)
+        multiply(last)
+
+        for i in range(len(banks)):
+            times_x(1, i)
+        for i, (j, n) in enumerate(banks):
+            add_skip_and_store(1, n, j, j + 1, nc.gpsimd if i == 0 else nc.vector)
+            turn_y(1, i)
+        for j, n in banks:
+            quantize_y(1, n, j, j + 1)

from contextlib import ExitStack

import concourse.mybir as mybir
from concourse.masks import make_identity

M, F, D = 512, 2048, 1024
FLOPS = 2 * 2 * M * F * D

F32 = mybir.dt.float32
BF16 = mybir.dt.bfloat16
I32 = mybir.dt.int32
U32 = mybir.dt.uint32
U8 = mybir.dt.uint8
FP8X4 = mybir.dt.float8_e4m3fn_x4
FP4X4 = mybir.dt.float4_e2m1fn_x4
ALU = mybir.AluOpType
ACT = mybir.ActivationFunctionType

P = 128
PACK = 4
GROUP = P * PACK
GROUPS = F // GROUP
HALF = 256
TILES = HALF // P
OUT_GROUPS = D // GROUP
PAIRS = (M // HALF) * GROUPS
PAIR_COLS = 2 * HALF
QUADRANTS = 4

ETA = 3.0 * 2.0 ** -21
LOG_FLOOR = 2.0 ** -60
ABS_MASK = 0x7FFF7FFF

LOWER_ON_GPSIMD = (416, 416, 416, 448, 512, 416, 384)
UPPER_ON_VECTOR = (384, 128, 0, 128, 0, 0, 0)


def tile_gated_block_relevance_step_g4_kernel(
    tc, rel, z_gate, z_up, share_gate, share_up, wg_words, wg_scales, wu_words, wu_scales, x, rel_skip,
    out_0, out_1, out_2,
):
    nc = tc.nc
    z_hbm = (z_gate, z_up)
    share_hbm = (share_gate, share_up)
    words_hbm = (wg_words, wu_words)
    scales_hbm = (wg_scales, wu_scales)

    with ExitStack() as ctx:
        keep = ctx.enter_context(tc.tile_pool(name="keep", bufs=1))
        work = ctx.enter_context(tc.tile_pool(name="work", bufs=3))
        turn = ctx.enter_context(tc.psum_pool(name="turn", bufs=4))
        sums = ctx.enter_context(tc.psum_pool(name="sums", bufs=1))
        ctx.enter_context(tc.manual_schedule())

        ident = keep.tile([P, P], F32, name="ident")
        log_floor = keep.tile([P, 1], F32, name="log_floor")
        w_scales = keep.tile([P, 2, GROUPS, D], U8, name="w_scales", align_bytes=64)
        w_words = keep.tile([P, 2, GROUPS, 2 * D], U8, name="w_words", align_bytes=64)
        share = [keep.tile([P, GROUPS, PACK], BF16, name="share%d" % b) for b in range(2)]
        pre = [keep.tile([P, 2, TILES, GROUP], BF16, name="pre%d" % q) for q in range(PAIRS)]
        rel_sb = [keep.tile([P, TILES, GROUP], BF16, name="rel%d" % q) for q in range(PAIRS)]
        x_sb = [keep.tile([P, TILES, D], BF16, name="x%d" % h) for h in range(2)]
        skip_sb = [keep.tile([P, TILES, D], BF16, name="skip%d" % h) for h in range(2)]
        y_codes = keep.tile([P, OUT_GROUPS, M], U32, name="y_codes", align_bytes=64)
        y_scales = keep.tile([P, OUT_GROUPS, M], U8, name="y_scales", align_bytes=64)
        share4 = [keep.tile([P, GROUPS, PACK], F32, name="share4_%d" % b) for b in range(2)]
        value = [keep.tile([P, PACK, PAIR_COLS], F32, name="value%d" % q) for q in range(PAIRS)]
        y_sb = [keep.tile([P, OUT_GROUPS, TILES, GROUP], F32, name="y%d" % h) for h in range(2)]
        lower_last = keep.tile([P, PAIR_COLS, PACK], BF16, name="lower_last", align_bytes=64)

        nc.vector.memset(log_floor[:], LOG_FLOOR)
        nc.vector.memset(w_scales[:].rearrange("p b g n -> p (b g n)").bitcast(I32), 0)
        make_identity(nc, ident[:])

        def token_rows(src, h, group):
            return src[h * HALF:(h + 1) * HALF, group * GROUP:(group + 1) * GROUP].rearrange("(j p) f -> p j f", p=P)

        rel_load_lag = 2
        for q in range(PAIRS + rel_load_lag):
            if q < PAIRS:
                for b in range(2):
                    nc.sync.dma_start(out=pre[q][:, b], in_=token_rows(z_hbm[b], q // GROUPS, q % GROUPS))
            if q >= rel_load_lag:
                r = q - rel_load_lag
                nc.sync.dma_start(out=rel_sb[r][:], in_=token_rows(rel, r // GROUPS, r % GROUPS))
        for b in range(2):
            nc.sync.dma_start(out=share[b][:], in_=share_hbm[b].rearrange("(g p t) -> p g t", p=P, t=PACK))
        for b in range(2):
            for quad in range(QUADRANTS):
                nc.sync.dma_start(
                    out=w_scales[32 * quad:32 * quad + 4, b, :, :].bitcast(I32),
                    in_=scales_hbm[b][:, 4 * quad:4 * quad + 4, :].rearrange("g r n -> r g n").bitcast(I32),
                )
        for g in range(GROUPS):
            for b in range(2):
                nc.sync.dma_start(out=w_words[:, b, g, :].bitcast(I32), in_=words_hbm[b][g].bitcast(I32))
        for h in range(2):
            tokens = slice(h * HALF, (h + 1) * HALF)
            nc.sync.dma_start(out=x_sb[h][:], in_=x[tokens, :].rearrange("(j p) f -> p j f", p=P))
            nc.sync.dma_start(out=skip_sb[h][:], in_=rel_skip[tokens, :].rearrange("(j p) f -> p j f", p=P))

        signed_t, upper, lower, codes, scales, acc, y_rounded = {}, {}, {}, {}, {}, {}, {}

        def flat(ap):
            return ap.rearrange("p a b -> p (a b)")

        def unit_cols(b):
            return slice(b * HALF, (b + 1) * HALF)

        def bank_values(bank):
            return flat(bank[:]).bitcast(BF16).rearrange("p (w k e) -> p w e k", w=2, e=2)

        def log_magnitude(q, b):
            magnitude = work.tile([P, TILES, 2, P], I32, name="magnitude", tag="magnitude")
            nc.vector.tensor_scalar(out=magnitude[:],
                                    in0=pre[q][:, b].bitcast(I32).rearrange("p j (c w) -> p j w c", w=2),
                                    scalar1=ABS_MASK, scalar2=None, op0=ALU.bitwise_and)
            bank = turn.tile([P, 2, HALF], F32, name="bank", tag="bank")
            for j in range(TILES):
                for w in range(2):
                    nc.tensor.transpose(bank[:, w, j * P:(j + 1) * P], magnitude[:, j, w, :].bitcast(F32), ident[:])
            nc.scalar.activation(out=value[q][:, :, unit_cols(b)].rearrange("p (w e) k -> p w e k", w=2),
                                 in_=bank_values(bank), func=ACT.Ln, bias=log_floor[:], scale=2.0)

        def half_sign(q):
            z = pre[q][:].rearrange("p b j f -> p (b j f)")
            nc.vector.tensor_scalar(out=z, in0=z, scalar1=0.0, scalar2=0.5, op0=ALU.is_ge, op1=ALU.subtract)

        def signed_rel(q):
            sign = pre[q][:].rearrange("p b j f -> p b (j f)")
            rel_twice = flat(rel_sb[q][:]).unsqueeze(1).to_broadcast([P, 2, TILES * GROUP])
            nc.vector.tensor_tensor(out=sign, in0=sign, in1=rel_twice, op=ALU.mult)

        def sigmoid(ap):
            nc.scalar.activation(out=ap, in_=ap, func=ACT.Sigmoid, scale=-1.0)

        def turn_signed_rel(q):
            for b in range(2):
                bank = turn.tile([P, 2, HALF], F32, name="bank", tag="bank")
                signed_t[q, b] = bank
                for j in range(TILES):
                    words = pre[q][:, b, j, :].bitcast(F32)
                    for w in range(2):
                        nc.tensor.transpose(bank[:, w, j * P:(j + 1) * P], words[:, w:GROUP // 2:2], ident[:])

        def message(q, b):
            signed = bank_values(signed_t[q, b])
            for t in range(PACK):
                plane = value[q][:, t, unit_cols(b)]
                nc.vector.scalar_tensor_tensor(out=plane, in0=plane, scalar=share4[b][:, q % GROUPS, t:t + 1],
                                               in1=signed[:, t // 2, t % 2, :], op0=ALU.mult, op1=ALU.mult)

        def round_scaled(dst, q, c0, c1, factor, engine):
            if engine == "gpsimd":
                nc.gpsimd.tensor_scalar(out=dst[:, c0:c1, :], in0=value[q][:, :, c0:c1].rearrange("p t k -> p k t"),
                                        scalar1=factor, scalar2=0.0, op0=ALU.mult, op1=ALU.add)
                return
            out = dst[:, c0:c1, :].rearrange("p (c i) t -> p c t i", i=4)
            src = value[q][:, :, c0:c1].rearrange("p t (c i) -> p c t i", i=4)
            if engine == "scalar":
                nc.scalar.activation(out=out, in_=src, func=ACT.Copy, scale=factor)
            else:
                nc.vector.tensor_scalar(out=out, in0=src, scalar1=factor, scalar2=None, op0=ALU.mult)

        def round_upper(q, c0, c1, engine):
            if c0 == 0:
                upper[q] = work.tile([P, PAIR_COLS, PACK], BF16, name="upper", tag="upper", bufs=2, align_bytes=64)
            if c0 < c1:
                round_scaled(upper[q], q, c0, c1, 0.5 * (1.0 + ETA), engine)

        def round_lower(q, c0, c1, engine):
            if c0 < c1:
                round_scaled(lower[q], q, c0, c1, 0.5 * (1.0 - ETA), engine)

        def round_lower_shared(q):
            lower[q] = work.tile([P, PAIR_COLS, PACK], BF16, name="lower", tag="lower", bufs=1, align_bytes=64)
            round_lower(q, LOWER_ON_GPSIMD[q], PAIR_COLS, "scalar")
            round_lower(q, 0, LOWER_ON_GPSIMD[q], "gpsimd")

        def join(q, b):
            total = flat(lower[q][:, unit_cols(b), :])
            nc.vector.tensor_tensor(out=total, in0=flat(upper[q][:, unit_cols(b), :]), in1=total, op=ALU.add)

        def quantize(q, b):
            if b == 0:
                codes[q] = work.tile([P, PAIR_COLS], U32, name="codes", tag="codes", align_bytes=64)
                scales[q] = work.tile([P, PAIR_COLS], U8, name="scales", tag="scales", align_bytes=64)
            nc.vector.quantize_mx(out=codes[q][:, unit_cols(b)].bitcast(FP8X4), scales=scales[q][:, unit_cols(b)],
                                  in_=flat(lower[q][:, unit_cols(b), :]))

        def join_and_quantize(q):
            for step in (join, quantize):
                for b in range(2):
                    step(q, b)

        banks = [(j, n) for n in range(OUT_GROUPS) for j in range(TILES)]

        def multiply(q):
            h, g = divmod(q, GROUPS)
            for i, (j, n) in enumerate(banks):
                if g == 0:
                    acc[h, i] = sums.tile([P, GROUP], F32, name="acc", tag="acc%d" % i)
                for b in range(2):
                    tokens = slice(b * HALF + j * P, b * HALF + (j + 1) * P)
                    nc.tensor.matmul_mx(
                        out=acc[h, i][:],
                        lhsT=codes[q][:, tokens].bitcast(FP8X4),
                        lhsT_scale=scales[q][:, tokens],
                        rhs=w_words[:, b, g, 2 * n * GROUP:2 * (n + 1) * GROUP].bitcast(FP4X4),
                        rhs_scale=w_scales[:, b, g, n * GROUP:(n + 1) * GROUP],
                        start=(g == 0 and b == 0),
                        stop=(g == GROUPS - 1 and b == 1),
                    )

        def times_x(h, i):
            j, n = banks[i]
            nc.vector.tensor_tensor(out=y_sb[h][:, n, j, :], in0=acc[h, i][:],
                                    in1=x_sb[h][:, j, n * GROUP:(n + 1) * GROUP], op=ALU.mult)

        def add_skip_and_store(h, n, j0, j1, engine):
            y = y_sb[h][:, n, j0:j1, :]
            engine.tensor_tensor(out=y, in0=y, in1=skip_sb[h][:, j0:j1, n * GROUP:(n + 1) * GROUP], op=ALU.add)
            nc.sync.dma_start(out=token_rows(out_0, h, n)[:, j0:j1, :], in_=y)

        def turn_y(h, i):
            j, n = banks[i]
            bank = turn.tile([P, PACK, P], F32, name="bank", tag="bank")
            for t in range(PACK):
                nc.tensor.transpose(bank[:, t, :], y_sb[h][:, n, j, t:GROUP:PACK], ident[:])
            if j == 0:
                y_rounded[h, n] = work.tile([P, HALF, PACK], BF16, name="y_rounded", tag="y_rounded", bufs=2,
                                            align_bytes=64)
            nc.scalar.copy(out=y_rounded[h, n][:, j * P:(j + 1) * P, :], in_=bank[:].rearrange("p t k -> p k t"))

        def quantize_y(h, n, j0, j1):
            tokens = slice(h * HALF + j0 * P, h * HALF + j1 * P)
            nc.vector.quantize_mx(out=y_codes[:, n, tokens].bitcast(FP8X4), scales=y_scales[:, n, tokens],
                                  in_=flat(y_rounded[h, n][:, j0 * P:j1 * P, :]))
            if j1 < TILES:
                return
            half = slice(h * HALF, (h + 1) * HALF)
            nc.sync.dma_start(out=out_1[n].rearrange("p m t -> p (m t)").bitcast(I32)[:, half],
                              in_=y_codes[:, n, half].bitcast(I32))
            if n == OUT_GROUPS - 1:
                for quad in range(QUADRANTS):
                    queue = nc.scalar if h == 1 and quad % 2 == 0 else nc.sync
                    queue.dma_start(
                        out=out_2[:, 4 * quad:4 * quad + 4, half].rearrange("g r m -> r g m").bitcast(I32),
                        in_=y_scales[32 * quad:32 * quad + 4, :, half].bitcast(I32),
                    )

        sign_lag, product_lag = 1, 3
        for q in range(PAIRS + product_lag):
            if q < PAIRS:
                log_magnitude(q, 0)
            if q >= product_lag:
                signed_rel(q - product_lag)
            if q < PAIRS:
                log_magnitude(q, 1)
            if 0 <= q - sign_lag < PAIRS:
                half_sign(q - sign_lag)
        for b in range(2):
            nc.vector.tensor_scalar(out=share4[b][:], in0=share[b][:], scalar1=4.0, scalar2=None, op0=ALU.mult)

        last = PAIRS - 1
        short_sigmoids = 2
        first_half_summed = GROUPS + 1
        sigmoid(value[0][:, 0:2, unit_cols(0)])
        sigmoid(value[0][:, 2:4, unit_cols(0)])
        sigmoid(value[0][:, :, unit_cols(1)])
        turn_signed_rel(0)
        for q in range(PAIRS):
            if q >= 2:
                round_upper(q - 2, PAIR_COLS - UPPER_ON_VECTOR[q - 2], PAIR_COLS, "vector")
                join_and_quantize(q - 2)
            if q > first_half_summed:
                add_skip_and_store(0, q - first_half_summed - 1, 0, TILES, nc.vector)
            if q >= 1:
                round_lower_shared(q - 1)
            if q + 1 <= short_sigmoids:
                for b in range(2):
                    sigmoid(value[q + 1][:, :, unit_cols(b)])
            elif q < last:
                sigmoid(flat(value[q + 1][:]))
            if q < last:
                turn_signed_rel(q + 1)
            if q >= 2:
                multiply(q - 2)
            message(q, 0)
            message(q, 1)
            if q == first_half_summed + 1:
                turn_y(0, 0)
            if q < last:
                round_upper(q, 0, PAIR_COLS - UPPER_ON_VECTOR[q], "scalar")
            if q == first_half_summed + 1:
                turn_y(0, 1)
            if q == first_half_summed:
                for i in range(len(banks)):
                    times_x(0, i)

        lower[last] = lower_last
        round_upper(last, 0, HALF, "scalar")
        round_lower(last, 0, HALF, "scalar")
        round_lower(last, HALF, PAIR_COLS, "scalar")
        join_and_quantize(last - 1)
        turn_y(0, 2)
        turn_y(0, 3)
        join(last, 0)
        round_upper(last, HALF, PAIR_COLS, "vector")
        quantize(last, 0)
        join(last, 1)
        quantize_y(0, 0, 0, TILES)
        quantize(last, 1)
        quantize_y(0, 1, 0, TILES)
        multiply(last - 1)
        multiply(last)

        for i in range(len(banks)):
            times_x(1, i)
        for i, (j, n) in enumerate(banks):
            add_skip_and_store(1, n, j, j + 1, nc.gpsimd if i == 0 else nc.vector)
            turn_y(1, i)
        for j, n in banks:
            quantize_y(1, n, j, j + 1)
